import numpy as np
import ml_dtypes


def mxq(x, axis, fmt="e4m3"):
    dtype, down = {"e4m3": (ml_dtypes.float8_e4m3fn, 7), "e5m2": (ml_dtypes.float8_e5m2, 14)}[fmt]
    v = np.moveaxis(np.asarray(x, np.float32).astype(ml_dtypes.bfloat16).astype(np.float64), axis, -1)
    blocks = v.reshape(v.shape[:-1] + (-1, 32))
    amax = np.abs(blocks).max(-1, keepdims=True)
    byte = np.maximum(np.where(amax > 0, np.frexp(amax)[1] - 1 + 127, 0) - down, 1)
    scale = np.exp2(byte - 127.0)
    codes = (blocks / scale).astype(np.float32).astype(dtype).astype(np.float64)
    return np.moveaxis((codes * scale).reshape(v.shape), -1, axis)


WIDE = False


def mx_kscale(k):
    if not WIDE:
        return np.ones(k)
    levels = np.array([10, -10, 5, -5, 0])
    if k % 512:
        return np.exp2(np.random.permutation(np.resize(levels, k // 32))).repeat(32)
    a = np.empty((k // 512, 16))
    for p in range(k // 512):
        a[p, :8] = np.random.permutation(np.resize(levels, 8))
        for g in range(8):
            far = levels[np.abs(levels - a[p, g]) >= 10]
            a[p, g + 8] = far[np.random.randint(len(far))]
    return np.exp2(a.ravel()).repeat(32)


def f64(x):
    return np.asarray(x).astype(np.float64)


def striped(idx):
    return np.tile(np.asarray(idx).reshape(-1, 16).T, (8, 1)).astype(np.uint16)


def unstriped(offs):
    return offs[:16].T.reshape(-1).astype(np.int64)


B, N, T, D, DV, NQ = 2, 512, 2048, 512, 256, 128
PAGE = 16


def setup_inputs():
    n = np.random.standard_normal
    pages = np.random.permutation(T // PAGE)[:B * N // PAGE]
    idx = (pages[:, None] * PAGE + np.arange(PAGE)[None, :]).reshape(-1)
    s = mx_kscale(D)[:, None]
    u = np.ones(T)
    u[idx] = mx_kscale(B * N)
    r = np.random.uniform(0.5, 2.0, T)
    k = n((D, T)) / s
    v = n((DV, T)) / (u * r)
    return {
        "qT": (n((B, D, NQ)) * s * (1.00 / np.sqrt(D))).astype(np.float32),
        "kT": k.astype(np.float32),
        "vT": v.astype(np.float32),
        "vs": np.tile(u * r, (128, 1)).astype(np.float32),
        "offs": striped(idx),
    }


def reference(qT, kT, vT, vs, offs):
    idx = unstriped(offs)
    k = f64(kT)
    v = f64(vT)
    pick = lambda x: x[:, idx].reshape(x.shape[0], B, N).transpose(1, 0, 2)
    q = f64(qT)
    score = mxq(q, 1, "e4m3").transpose(0, 2, 1) @ mxq(pick(k), 1, "e4m3")
    p = score / (1.0 + np.exp(-score))
    w = p * pick(f64(vs))[:, :1, :]
    y = mxq(w, 2, "e4m3") @ mxq(pick(v).transpose(0, 2, 1), 1, "e4m3")
    y = y / 16.0
    return y

@@ -1,0 +1,245 @@
+from contextlib import ExitStack
+
+import concourse.mybir as mybir
+from concourse.masks import make_identity
+
+B, N, T, D, DV, NQ = 2, 512, 2048, 512, 256, 128
+P = 128
+PACK = 4
+PAIRS = 2
+E_BLOCKS = DV // P
+LIST_COLS = N // 16
+CHUNKS = 4
+CHUNK = T // CHUNKS
+FLOPS = 2 * B * NQ * N * (D + DV)
+
+F32 = mybir.dt.float32
+BF16 = mybir.dt.bfloat16
+U32 = mybir.dt.uint32
+U16 = mybir.dt.uint16
+U8 = mybir.dt.uint8
+FP8X4 = mybir.dt.float8_e4m3fn_x4
+COPY = mybir.ActivationFunctionType.Copy
+SILU = mybir.ActivationFunctionType.Silu
+MULT = mybir.AluOpType.mult
+
+VECTOR_CASTS = {(0, 3), (1, 1), (1, 3)}
+
+
+def tile_attend_x_silu_kernel(tc, qT, kT, vT, vs, offs, out):
+    nc = tc.nc
+    with ExitStack() as ctx:
+        keep = ctx.enter_context(tc.tile_pool(name="keep", bufs=1))
+        turn_pool = ctx.enter_context(tc.psum_pool(name="turn", bufs=4))
+        score_pool = ctx.enter_context(tc.psum_pool(name="score", bufs=2))
+        out_pool = ctx.enter_context(tc.psum_pool(name="outs", bufs=2))
+
+        lists = keep.tile([P, B * LIST_COLS], U16, name="lists")
+        nc.sync.dma_start(lists[:], offs)
+
+        identity = keep.tile([P, P], F32, name="identity")
+        make_identity(nc, identity[:])
+        vs_row = keep.tile([P, T], F32, name="vs_row")
+        nc.gpsimd.memset(vs_row[:], 0.0)
+
+        warm = keep.tile([P, 1], F32, name="warm")
+        nc.vector.memset(warm[:], 0.0)
+        nc.scalar.activation(warm[:], warm[:], SILU)
+
+        k_rows = kT.rearrange("(p j) w -> p j w", j=PACK)
+        k_raw = {}
+
+        def load_keys(pair):
+            for c in range(CHUNKS):
+                raw = keep.tile([P, 2, CHUNK], F32, name=f"k_raw_{pair}_{c}")
+                nc.sync.dma_start(raw[:], k_rows[:, 2 * pair : 2 * pair + 2, c * CHUNK : (c + 1) * CHUNK])
+                k_raw[pair, c] = raw
+
+        load_keys(0)
+        q_raw = keep.tile([P, B, PACK, NQ], F32, name="q_raw")
+        nc.sync.dma_start(q_raw[:], qT.rearrange("b (p j) q -> p b j q", j=PACK))
+        nc.sync.dma_start(vs_row[0:1, :], vs[0:1, :])
+        load_keys(1)
+        v_raw = []
+        for e in range(E_BLOCKS):
+            raw = keep.tile([P, T], F32, name=f"v_raw_{e}")
+            nc.sync.dma_start(raw[:], vT[e * P : (e + 1) * P, :])
+            v_raw.append(raw)
+
+        k_pairs = []
+        for pair in range(PAIRS):
+            k_pair = keep.tile([P, T * 2], BF16, name=f"k_pair_{pair}")
+            k_pairs.append(k_pair)
+        k_groups = []
+        for b in range(B):
+            k_group = keep.tile([P, N * PACK], BF16, name=f"k_group_{b}", align_bytes=64)
+            k_groups.append(k_group)
+
+        def cast_keys(pair):
+            for c in range(CHUNKS):
+                dst = k_pairs[pair][:, c * CHUNK * 2 : (c + 1) * CHUNK * 2].rearrange("p (w j) -> p w j", j=2)
+                src = k_raw[pair, c][:].rearrange("p j w -> p w j")
+                if (pair, c) in VECTOR_CASTS:
+                    nc.vector.tensor_copy(dst, src)
+                else:
+                    nc.scalar.activation(dst, src, COPY)
+
+        def offsets(b):
+            return lists[:, b * LIST_COLS : (b + 1) * LIST_COLS]
+
+        def gather_keys(pair, b):
+            words = k_groups[b][:].bitcast(U32).rearrange("p (t s u) -> p u s t", t=PACK, u=PAIRS)
+            nc.vector.tensor_copy(words[:, pair], k_pairs[pair][:].bitcast(U32).indirect(offsets(b)))
+
+        cast_keys(0)
+
+        q_group = keep.tile([P, B * NQ * PACK], BF16, name="q_group", align_bytes=64)
+        nc.vector.tensor_copy(
+            q_group[:].rearrange("p (b q j) -> p b q j", b=B, j=PACK), q_raw[:].rearrange("p b j q -> p b q j")
+        )
+        gather_keys(0, 0)
+        q_codes = keep.tile([P, B * NQ], U32, name="q_codes", align_bytes=64)
+        q_scales = keep.tile([P, B * NQ], U8, name="q_scales", align_bytes=64)
+        nc.vector.quantize_mx(out=q_codes[:].bitcast(FP8X4), scales=q_scales[:], in_=q_group[:])
+        gather_keys(0, 1)
+
+        vs_slots = keep.tile([P, B * N], F32, name="vs_slots")
+        nc.vector.tensor_copy(vs_slots[:], vs_row[:].indirect(lists[:]))
+        vs_cols = []
+        for b in range(B):
+            turned = turn_pool.tile([P, PACK, P], F32, name="turned")
+            for t in range(PACK):
+                nc.tensor.transpose(turned[:, t, :], vs_slots[:, b * N + t : (b + 1) * N : PACK], identity[:])
+            col = keep.tile([P, PACK], F32, name=f"vs_col_{b}")
+            nc.scalar.activation(col[:], turned[:, :, 0], COPY)
+            vs_cols.append(col)
+
+        cast_keys(1)
+
+        k_codes = []
+        k_scales = []
+        for b in range(B):
+            codes = keep.tile([P, N], U32, name=f"k_codes_{b}", align_bytes=64)
+            scales = keep.tile([P, N], U8, name=f"k_scales_{b}", align_bytes=64)
+            k_codes.append(codes)
+            k_scales.append(scales)
+
+        def quantise_keys(b):
+            nc.vector.quantize_mx(out=k_codes[b][:].bitcast(FP8X4), scales=k_scales[b][:], in_=k_groups[b][:])
+
+        probs = {}
+
+        def scores(b):
+            acc = score_pool.tile([P, PACK, NQ], F32, name="acc")
+            for t in range(PACK):
+                s = slice(t * P, (t + 1) * P)
+                q = slice(b * NQ, (b + 1) * NQ)
+                nc.tensor.matmul_mx(
+                    out=acc[:, t, :],
+                    lhsT=k_codes[b][:, s].bitcast(FP8X4),
+                    lhsT_scale=k_scales[b][:, s],
+                    rhs=q_codes[:, q].bitcast(FP8X4),
+                    rhs_scale=q_scales[:, q],
+                    start=True,
+                    stop=True,
+                )
+            prob = keep.tile([P, PACK, NQ], F32, name=f"prob_{b}")
+            nc.scalar.activation(prob[:], acc[:], SILU)
+            probs[b] = prob
+
+        w_groups = {}
+        w_codes = {}
+        w_scales = {}
+
+        def weigh(b):
+            w_group = keep.tile([P, NQ, PACK], BF16, name=f"w_group_{b}", align_bytes=64)
+            nc.vector.tensor_tensor(
+                w_group[:],
+                probs[b][:].rearrange("p t q -> p q t"),
+                vs_cols[b][:].unsqueeze(1).to_broadcast([P, NQ, PACK]),
+                MULT,
+            )
+            w_groups[b] = w_group
+
+        def quantise_weights(b):
+            codes = keep.tile([P, NQ], U32, name=f"w_codes_{b}", align_bytes=64)
+            scales = keep.tile([P, NQ], U8, name=f"w_scales_{b}", align_bytes=64)
+            nc.vector.quantize_mx(
+                out=codes[:].bitcast(FP8X4), scales=scales[:], in_=w_groups[b][:].rearrange("p q t -> p (q t)")
+            )
+            w_codes[b] = codes
+            w_scales[b] = scales
+
+        v_slots = {}
+        v_groups = {}
+        v_codes = {}
+        v_scales = {}
+
+        def gather_values(e, b):
+            slots = keep.tile([P, N], F32, name=f"v_slots_{e}_{b}")
+            nc.vector.tensor_copy(slots[:], v_raw[e][:].indirect(offsets(b)))
+            v_slots[e, b] = slots
+
+        def turn_values(e, b):
+            turned = turn_pool.tile([P, PACK, P], F32, name="turned")
+            for t in range(PACK):
+                nc.tensor.transpose(turned[:, t, :], v_slots[e, b][:, t:N:PACK], identity[:])
+            group = keep.tile([P, P, PACK], BF16, name=f"v_group_{e}_{b}", align_bytes=64)
+            nc.scalar.activation(group[:], turned[:].rearrange("p t e -> p e t"), COPY)
+            v_groups[e, b] = group
+
+        def quantise_values(e, b):
+            codes = keep.tile([P, P], U32, name=f"v_codes_{e}_{b}", align_bytes=64)
+            scales = keep.tile([P, P], U8, name=f"v_scales_{e}_{b}", align_bytes=64)
+            nc.vector.quantize_mx(
+                out=codes[:].bitcast(FP8X4), scales=scales[:], in_=v_groups[e, b][:].rearrange("p e t -> p (e t)")
+            )
+            v_codes[e, b] = codes
+            v_scales[e, b] = scales
+
+        sums = {}
+
+        def finish(e, b):
+            if b not in sums:
+                total = out_pool.tile([P, DV], F32, name="total")
+                sums[b] = total
+            cols = slice(e * P, (e + 1) * P)
+            nc.tensor.matmul_mx(
+                out=sums[b][:, cols],
+                lhsT=w_codes[b][:].bitcast(FP8X4),
+                lhsT_scale=w_scales[b][:],
+                rhs=v_codes[e, b][:].bitcast(FP8X4),
+                rhs_scale=v_scales[e, b][:],
+                start=True,
+                stop=True,
+            )
+            result = keep.tile([P, P], F32, name=f"result_{e}_{b}")
+            nc.scalar.activation(result[:], sums[b][:, cols], COPY, scale=1.0 / 16.0)
+            nc.sync.dma_start(out[b, :, cols], result[:])
+
+        gather_keys(1, 0)
+        gather_keys(1, 1)
+        quantise_keys(0)
+        scores(0)
+        quantise_keys(1)
+        scores(1)
+        gather_values(0, 0)
+        weigh(0)
+        gather_values(0, 1)
+        quantise_weights(0)
+        weigh(1)
+        turn_values(0, 0)
+        quantise_values(0, 0)
+        quantise_weights(1)
+        turn_values(0, 1)
+        finish(0, 0)
+        quantise_values(0, 1)
+        finish(0, 1)
+        gather_values(1, 0)
+        turn_values(1, 0)
+        gather_values(1, 1)
+        turn_values(1, 1)
+        quantise_values(1, 0)
+        finish(1, 0)
+        quantise_values(1, 1)
+        finish(1, 1)

@@ -9,8 +9,8 @@ PACK = 4
 PAIRS = 2
 E_BLOCKS = DV // P
 LIST_COLS = N // 16
-CHUNKS = 4
-CHUNK = T // CHUNKS
+
+SHARES = (((1024, 0), (640, 384)), ((768, 256), (512, 0), (256, 256)))
 FLOPS = 2 * B * NQ * N * (D + DV)
 
 F32 = mybir.dt.float32
@@ -22,8 +22,6 @@ FP8X4 = mybir.dt.float8_e4m3fn_x4
 COPY = mybir.ActivationFunctionType.Copy
 SILU = mybir.ActivationFunctionType.Silu
 MULT = mybir.AluOpType.mult
-
-VECTOR_CASTS = {(0, 3), (1, 1), (1, 3)}
 
 
 def tile_attend_x_silu_kernel(tc, qT, kT, vT, vs, offs, out):
@@ -40,7 +38,7 @@ def tile_attend_x_silu_kernel(tc, qT, kT, vT, vs, offs, out):
         identity = keep.tile([P, P], F32, name="identity")
         make_identity(nc, identity[:])
         vs_row = keep.tile([P, T], F32, name="vs_row")
-        nc.gpsimd.memset(vs_row[:], 0.0)
+        nc.vector.memset(vs_row[:], 0.0)
 
         warm = keep.tile([P, 1], F32, name="warm")
         nc.vector.memset(warm[:], 0.0)
@@ -50,21 +48,28 @@ def tile_attend_x_silu_kernel(tc, qT, kT, vT, vs, offs, out):
         k_raw = {}
 
         def load_keys(pair):
-            for c in range(CHUNKS):
-                raw = keep.tile([P, 2, CHUNK], F32, name=f"k_raw_{pair}_{c}")
-                nc.sync.dma_start(raw[:], k_rows[:, 2 * pair : 2 * pair + 2, c * CHUNK : (c + 1) * CHUNK])
+            start = 0
+            for c, (on_scalar, on_vector) in enumerate(SHARES[pair]):
+                width = on_scalar + on_vector
+                raw = keep.tile([P, 2, width], F32, name=f"k_raw_{pair}_{c}")
+                nc.sync.dma_start(raw[:], k_rows[:, 2 * pair : 2 * pair + 2, start : start + width])
                 k_raw[pair, c] = raw
+                start += width
 
-        load_keys(0)
-        q_raw = keep.tile([P, B, PACK, NQ], F32, name="q_raw")
-        nc.sync.dma_start(q_raw[:], qT.rearrange("b (p j) q -> p b j q", j=PACK))
-        nc.sync.dma_start(vs_row[0:1, :], vs[0:1, :])
-        load_keys(1)
         v_raw = []
-        for e in range(E_BLOCKS):
+
+        def load_values(e):
             raw = keep.tile([P, T], F32, name=f"v_raw_{e}")
             nc.sync.dma_start(raw[:], vT[e * P : (e + 1) * P, :])
             v_raw.append(raw)
+
+        load_values(0)
+        nc.sync.dma_start(vs_row[0:1, :], vs[0:1, :])
+        load_keys(0)
+        q_raw = keep.tile([P, B, PACK, NQ], F32, name="q_raw")
+        nc.sync.dma_start(q_raw[:], qT.rearrange("b (p j) q -> p b j q", j=PACK))
+        load_keys(1)
+        load_values(1)
 
         k_pairs = []
         for pair in range(PAIRS):
@@ -76,13 +81,15 @@ def tile_attend_x_silu_kernel(tc, qT, kT, vT, vs, offs, out):
             k_groups.append(k_group)
 
         def cast_keys(pair):
-            for c in range(CHUNKS):
-                dst = k_pairs[pair][:, c * CHUNK * 2 : (c + 1) * CHUNK * 2].rearrange("p (w j) -> p w j", j=2)
+            start = 0
+            for c, (on_scalar, on_vector) in enumerate(SHARES[pair]):
+                width = on_scalar + on_vector
+                dst = k_pairs[pair][:, 2 * start : 2 * (start + width)].rearrange("p (w j) -> p w j", j=2)
                 src = k_raw[pair, c][:].rearrange("p j w -> p w j")
-                if (pair, c) in VECTOR_CASTS:
-                    nc.vector.tensor_copy(dst, src)
-                else:
-                    nc.scalar.activation(dst, src, COPY)
+                nc.scalar.activation(dst[:, :on_scalar], src[:, :on_scalar], COPY)
+                if on_vector:
+                    nc.vector.tensor_copy(dst[:, on_scalar:], src[:, on_scalar:])
+                start += width
 
         def offsets(b):
             return lists[:, b * LIST_COLS : (b + 1) * LIST_COLS]
@@ -91,30 +98,28 @@ def tile_attend_x_silu_kernel(tc, qT, kT, vT, vs, offs, out):
             words = k_groups[b][:].bitcast(U32).rearrange("p (t s u) -> p u s t", t=PACK, u=PAIRS)
             nc.vector.tensor_copy(words[:, pair], k_pairs[pair][:].bitcast(U32).indirect(offsets(b)))
 
-        cast_keys(0)
-
         q_group = keep.tile([P, B * NQ * PACK], BF16, name="q_group", align_bytes=64)
-        nc.vector.tensor_copy(
-            q_group[:].rearrange("p (b q j) -> p b q j", b=B, j=PACK), q_raw[:].rearrange("p b j q -> p b q j")
-        )
-        gather_keys(0, 0)
         q_codes = keep.tile([P, B * NQ], U32, name="q_codes", align_bytes=64)
         q_scales = keep.tile([P, B * NQ], U8, name="q_scales", align_bytes=64)
-        nc.vector.quantize_mx(out=q_codes[:].bitcast(FP8X4), scales=q_scales[:], in_=q_group[:])
-        gather_keys(0, 1)
 
-        vs_slots = keep.tile([P, B * N], F32, name="vs_slots")
-        nc.vector.tensor_copy(vs_slots[:], vs_row[:].indirect(lists[:]))
+        def queries():
+            nc.vector.tensor_copy(
+                q_group[:].rearrange("p (b q j) -> p b q j", b=B, j=PACK), q_raw[:].rearrange("p b j q -> p b q j")
+            )
+            nc.vector.quantize_mx(out=q_codes[:].bitcast(FP8X4), scales=q_scales[:], in_=q_group[:])
+
         vs_cols = []
-        for b in range(B):
-            turned = turn_pool.tile([P, PACK, P], F32, name="turned")
-            for t in range(PACK):
-                nc.tensor.transpose(turned[:, t, :], vs_slots[:, b * N + t : (b + 1) * N : PACK], identity[:])
-            col = keep.tile([P, PACK], F32, name=f"vs_col_{b}")
-            nc.scalar.activation(col[:], turned[:, :, 0], COPY)
-            vs_cols.append(col)
 
-        cast_keys(1)
+        def token_scales():
+            vs_slots = keep.tile([P, B * N], F32, name="vs_slots")
+            nc.vector.tensor_copy(vs_slots[:], vs_row[:].indirect(lists[:]))
+            for b in range(B):
+                turned = turn_pool.tile([P, PACK, P], F32, name="turned")
+                for t in range(PACK):
+                    nc.tensor.transpose(turned[:, t, :], vs_slots[:, b * N + t : (b + 1) * N : PACK], identity[:])
+                col = keep.tile([P, PACK], F32, name=f"vs_col_{b}")
+                nc.scalar.activation(col[:], turned[:, :, 0], COPY)
+                vs_cols.append(col)
 
         k_codes = []
         k_scales = []
@@ -217,26 +222,32 @@ def tile_attend_x_silu_kernel(tc, qT, kT, vT, vs, offs, out):
             nc.scalar.activation(result[:], sums[b][:, cols], COPY, scale=1.0 / 16.0)
             nc.sync.dma_start(out[b, :, cols], result[:])
 
+        gather_values(0, 0)
+        turn_values(0, 0)
+        gather_values(0, 1)
+        turn_values(0, 1)
+        token_scales()
+        quantise_values(0, 0)
+        quantise_values(0, 1)
+        cast_keys(0)
+        queries()
+        gather_keys(0, 0)
+        gather_keys(0, 1)
+        cast_keys(1)
         gather_keys(1, 0)
-        gather_keys(1, 1)
         quantise_keys(0)
         scores(0)
+        gather_keys(1, 1)
         quantise_keys(1)
         scores(1)
-        gather_values(0, 0)
         weigh(0)
-        gather_values(0, 1)
         quantise_weights(0)
-        weigh(1)
-        turn_values(0, 0)
-        quantise_values(0, 0)
-        quantise_weights(1)
-        turn_values(0, 1)
         finish(0, 0)
-        quantise_values(0, 1)
-        finish(0, 1)
         gather_values(1, 0)
         turn_values(1, 0)
+        weigh(1)
+        quantise_weights(1)
+        finish(0, 1)
         gather_values(1, 1)
         turn_values(1, 1)
         quantise_values(1, 0)

@@ -6,11 +6,7 @@ from concourse.masks import make_identity
 B, N, T, D, DV, NQ = 2, 512, 2048, 512, 256, 128
 P = 128
 PACK = 4
-PAIRS = 2
-E_BLOCKS = DV // P
 LIST_COLS = N // 16
-
-SHARES = (((1024, 0), (640, 384)), ((768, 256), (512, 0), (256, 256)))
 FLOPS = 2 * B * NQ * N * (D + DV)
 
 F32 = mybir.dt.float32
@@ -23,23 +19,26 @@ COPY = mybir.ActivationFunctionType.Copy
 SILU = mybir.ActivationFunctionType.Silu
 MULT = mybir.AluOpType.mult
 
+K_SHARES = (((448, 64), (448, 64), (640, 384)), ((832, 192), (192, 320), (320, 192)))
+
 
 def tile_attend_x_silu_kernel(tc, qT, kT, vT, vs, offs, out):
     nc = tc.nc
     with ExitStack() as ctx:
         keep = ctx.enter_context(tc.tile_pool(name="keep", bufs=1))
-        turn_pool = ctx.enter_context(tc.psum_pool(name="turn", bufs=4))
+        scale_pool = ctx.enter_context(tc.psum_pool(name="scale", bufs=2))
+        turn_pool = ctx.enter_context(tc.psum_pool(name="turn", bufs=2))
         score_pool = ctx.enter_context(tc.psum_pool(name="score", bufs=2))
         out_pool = ctx.enter_context(tc.psum_pool(name="outs", bufs=2))
 
         lists = keep.tile([P, B * LIST_COLS], U16, name="lists")
         nc.sync.dma_start(lists[:], offs)
 
+        vs_row = keep.tile([P, T], F32, name="vs_row")
+        nc.vector.memset(vs_row[:, : T // 2], 0.0)
+        nc.gpsimd.memset(vs_row[:, T // 2 :], 0.0)
         identity = keep.tile([P, P], F32, name="identity")
         make_identity(nc, identity[:])
-        vs_row = keep.tile([P, T], F32, name="vs_row")
-        nc.vector.memset(vs_row[:], 0.0)
-
         warm = keep.tile([P, 1], F32, name="warm")
         nc.vector.memset(warm[:], 0.0)
         nc.scalar.activation(warm[:], warm[:], SILU)
@@ -47,210 +46,214 @@ def tile_attend_x_silu_kernel(tc, qT, kT, vT, vs, offs, out):
         k_rows = kT.rearrange("(p j) w -> p j w", j=PACK)
         k_raw = {}
 
-        def load_keys(pair):
-            start = 0
-            for c, (on_scalar, on_vector) in enumerate(SHARES[pair]):
-                width = on_scalar + on_vector
-                raw = keep.tile([P, 2, width], F32, name=f"k_raw_{pair}_{c}")
-                nc.sync.dma_start(raw[:], k_rows[:, 2 * pair : 2 * pair + 2, start : start + width])
-                k_raw[pair, c] = raw
-                start += width
+        def load_keys(u, c):
+            start = sum(a + b for a, b in K_SHARES[u][:c])
+            width = sum(K_SHARES[u][c])
+            raw = keep.tile([P, 2, width], F32, name=f"k_raw_{u}_{c}")
+            nc.sync.dma_start(raw[:], k_rows[:, 2 * u : 2 * u + 2, start : start + width])
+            k_raw[u, c] = raw
 
-        v_raw = []
+        v_raw = {}
 
         def load_values(e):
             raw = keep.tile([P, T], F32, name=f"v_raw_{e}")
             nc.sync.dma_start(raw[:], vT[e * P : (e + 1) * P, :])
-            v_raw.append(raw)
+            v_raw[e] = raw
 
-        load_values(0)
-        nc.sync.dma_start(vs_row[0:1, :], vs[0:1, :])
-        load_keys(0)
         q_raw = keep.tile([P, B, PACK, NQ], F32, name="q_raw")
         nc.sync.dma_start(q_raw[:], qT.rearrange("b (p j) q -> p b j q", j=PACK))
-        load_keys(1)
+        load_keys(0, 0)
+        nc.sync.dma_start(vs_row[0:1, :], vs[0:1, :])
+        load_keys(0, 1)
+        load_keys(0, 2)
+        load_keys(1, 0)
+        load_keys(1, 1)
+        load_keys(1, 2)
+        load_values(0)
         load_values(1)
 
         k_pairs = []
-        for pair in range(PAIRS):
-            k_pair = keep.tile([P, T * 2], BF16, name=f"k_pair_{pair}")
-            k_pairs.append(k_pair)
-        k_groups = []
-        for b in range(B):
-            k_group = keep.tile([P, N * PACK], BF16, name=f"k_group_{b}", align_bytes=64)
-            k_groups.append(k_group)
+        for u in range(2):
+            pair = keep.tile([P, T * 2], BF16, name=f"k_pair_{u}")
+            k_pairs.append(pair)
 
-        def cast_keys(pair):
-            start = 0
-            for c, (on_scalar, on_vector) in enumerate(SHARES[pair]):
-                width = on_scalar + on_vector
-                dst = k_pairs[pair][:, 2 * start : 2 * (start + width)].rearrange("p (w j) -> p w j", j=2)
-                src = k_raw[pair, c][:].rearrange("p j w -> p w j")
+        def cast_keys(u, c):
+            start = sum(a + b for a, b in K_SHARES[u][:c])
+            on_scalar, on_vector = K_SHARES[u][c]
+            dst = k_pairs[u][:, 2 * start : 2 * (start + on_scalar + on_vector)].rearrange("p (w j) -> p w j", j=2)
+            src = k_raw[u, c][:].rearrange("p j w -> p w j")
+            if on_scalar:
                 nc.scalar.activation(dst[:, :on_scalar], src[:, :on_scalar], COPY)
-                if on_vector:
-                    nc.vector.tensor_copy(dst[:, on_scalar:], src[:, on_scalar:])
-                start += width
+            if on_vector:
+                nc.vector.tensor_copy(dst[:, on_scalar:], src[:, on_scalar:])
 
         def offsets(b):
             return lists[:, b * LIST_COLS : (b + 1) * LIST_COLS]
 
-        def gather_keys(pair, b):
-            words = k_groups[b][:].bitcast(U32).rearrange("p (t s u) -> p u s t", t=PACK, u=PAIRS)
-            nc.vector.tensor_copy(words[:, pair], k_pairs[pair][:].bitcast(U32).indirect(offsets(b)))
+        k_slots = keep.tile([P, 2 * B * N], U32, name="k_slots")
+        k_words = k_slots[:].rearrange("p (u b t s) -> p u b s t", u=2, b=B, t=PACK)
+        k_groups = []
+        for b in range(B):
+            group = keep.tile([P, N * PACK], BF16, name=f"k_group_{b}", align_bytes=64)
+            k_groups.append(group)
 
-        q_group = keep.tile([P, B * NQ * PACK], BF16, name="q_group", align_bytes=64)
-        q_codes = keep.tile([P, B * NQ], U32, name="q_codes", align_bytes=64)
-        q_scales = keep.tile([P, B * NQ], U8, name="q_scales", align_bytes=64)
-
-        def queries():
-            nc.vector.tensor_copy(
-                q_group[:].rearrange("p (b q j) -> p b q j", b=B, j=PACK), q_raw[:].rearrange("p b j q -> p b q j")
+        def interleave_keys(b):
+            nc.scalar.copy(
+                k_groups[b][:].rearrange("p (n u j) -> p n u j", u=2, j=2),
+                k_slots[:].bitcast(BF16).rearrange("p (u b n j) -> p b n u j", u=2, b=B, j=2)[:, b],
             )
-            nc.vector.quantize_mx(out=q_codes[:].bitcast(FP8X4), scales=q_scales[:], in_=q_group[:])
 
-        vs_cols = []
+        def quantise(name, values, columns):
+            codes = keep.tile([P, columns], U32, name=f"{name}_codes", align_bytes=64)
+            scales = keep.tile([P, columns], U8, name=f"{name}_scales", align_bytes=64)
+            nc.vector.quantize_mx(out=codes[:].bitcast(FP8X4), scales=scales[:], in_=values)
+            return codes, scales
+
+        mx = {}
+        probs = {}
+        w_groups = {}
+        vs_turned = {}
 
         def token_scales():
             vs_slots = keep.tile([P, B * N], F32, name="vs_slots")
             nc.vector.tensor_copy(vs_slots[:], vs_row[:].indirect(lists[:]))
             for b in range(B):
-                turned = turn_pool.tile([P, PACK, P], F32, name="turned")
+                turned = scale_pool.tile([P, PACK, P], F32, name="scale_turned")
                 for t in range(PACK):
                     nc.tensor.transpose(turned[:, t, :], vs_slots[:, b * N + t : (b + 1) * N : PACK], identity[:])
-                col = keep.tile([P, PACK], F32, name=f"vs_col_{b}")
-                nc.scalar.activation(col[:], turned[:, :, 0], COPY)
-                vs_cols.append(col)
+                vs_turned[b] = turned
 
-        k_codes = []
-        k_scales = []
-        for b in range(B):
-            codes = keep.tile([P, N], U32, name=f"k_codes_{b}", align_bytes=64)
-            scales = keep.tile([P, N], U8, name=f"k_scales_{b}", align_bytes=64)
-            k_codes.append(codes)
-            k_scales.append(scales)
+        q_group = keep.tile([P, B * NQ * PACK], BF16, name="q_group", align_bytes=64)
+
+        def round_queries():
+            nc.gpsimd.tensor_scalar(
+                q_group[:].rearrange("p (b q j) -> p b q j", b=B, j=PACK),
+                q_raw[:].rearrange("p b j q -> p b q j"),
+                1.0,
+                0.0,
+                MULT,
+                mybir.AluOpType.add,
+            )
+
+        def quantise_queries():
+            mx["q"] = quantise("q", q_group[:], B * NQ)
+
+        def gather_keys(u, b):
+            nc.vector.tensor_copy(k_words[:, u, b], k_pairs[u][:].bitcast(U32).indirect(offsets(b)))
 
         def quantise_keys(b):
-            nc.vector.quantize_mx(out=k_codes[b][:].bitcast(FP8X4), scales=k_scales[b][:], in_=k_groups[b][:])
+            mx["k", b] = quantise(f"k_{b}", k_groups[b][:], N)
 
-        probs = {}
+        def multiply(out_cols, left, left_cols, right, right_cols):
+            nc.tensor.matmul_mx(
+                out=out_cols,
+                lhsT=left[0][:, left_cols].bitcast(FP8X4),
+                lhsT_scale=left[1][:, left_cols],
+                rhs=right[0][:, right_cols].bitcast(FP8X4),
+                rhs_scale=right[1][:, right_cols],
+                start=True,
+                stop=True,
+            )
+
+        def block(i):
+            return slice(i * P, (i + 1) * P)
 
         def scores(b):
             acc = score_pool.tile([P, PACK, NQ], F32, name="acc")
             for t in range(PACK):
-                s = slice(t * P, (t + 1) * P)
-                q = slice(b * NQ, (b + 1) * NQ)
-                nc.tensor.matmul_mx(
-                    out=acc[:, t, :],
-                    lhsT=k_codes[b][:, s].bitcast(FP8X4),
-                    lhsT_scale=k_scales[b][:, s],
-                    rhs=q_codes[:, q].bitcast(FP8X4),
-                    rhs_scale=q_scales[:, q],
-                    start=True,
-                    stop=True,
-                )
+                multiply(acc[:, t, :], mx["k", b], block(t), mx["q"], block(b))
             prob = keep.tile([P, PACK, NQ], F32, name=f"prob_{b}")
             nc.scalar.activation(prob[:], acc[:], SILU)
             probs[b] = prob
 
-        w_groups = {}
-        w_codes = {}
-        w_scales = {}
-
         def weigh(b):
-            w_group = keep.tile([P, NQ, PACK], BF16, name=f"w_group_{b}", align_bytes=64)
+            group = keep.tile([P, NQ, PACK], BF16, name=f"w_group_{b}", align_bytes=64)
             nc.vector.tensor_tensor(
-                w_group[:],
+                group[:],
                 probs[b][:].rearrange("p t q -> p q t"),
-                vs_cols[b][:].unsqueeze(1).to_broadcast([P, NQ, PACK]),
+                vs_turned[b][:, :, 0].unsqueeze(1).to_broadcast([P, NQ, PACK]),
                 MULT,
             )
-            w_groups[b] = w_group
+            w_groups[b] = group
 
         def quantise_weights(b):
-            codes = keep.tile([P, NQ], U32, name=f"w_codes_{b}", align_bytes=64)
-            scales = keep.tile([P, NQ], U8, name=f"w_scales_{b}", align_bytes=64)
-            nc.vector.quantize_mx(
-                out=codes[:].bitcast(FP8X4), scales=scales[:], in_=w_groups[b][:].rearrange("p q t -> p (q t)")
-            )
-            w_codes[b] = codes
-            w_scales[b] = scales
+            mx["w", b] = quantise(f"w_{b}", w_groups[b][:].rearrange("p q t -> p (q t)"), NQ)
 
-        v_slots = {}
-        v_groups = {}
-        v_codes = {}
-        v_scales = {}
-
-        def gather_values(e, b):
-            slots = keep.tile([P, N], F32, name=f"v_slots_{e}_{b}")
-            nc.vector.tensor_copy(slots[:], v_raw[e][:].indirect(offsets(b)))
-            v_slots[e, b] = slots
-
-        def turn_values(e, b):
+        def turn_values(slots, group):
             turned = turn_pool.tile([P, PACK, P], F32, name="turned")
             for t in range(PACK):
-                nc.tensor.transpose(turned[:, t, :], v_slots[e, b][:, t:N:PACK], identity[:])
-            group = keep.tile([P, P, PACK], BF16, name=f"v_group_{e}_{b}", align_bytes=64)
-            nc.scalar.activation(group[:], turned[:].rearrange("p t e -> p e t"), COPY)
-            v_groups[e, b] = group
-
-        def quantise_values(e, b):
-            codes = keep.tile([P, P], U32, name=f"v_codes_{e}_{b}", align_bytes=64)
-            scales = keep.tile([P, P], U8, name=f"v_scales_{e}_{b}", align_bytes=64)
-            nc.vector.quantize_mx(
-                out=codes[:].bitcast(FP8X4), scales=scales[:], in_=v_groups[e, b][:].rearrange("p e t -> p (e t)")
+                nc.tensor.transpose(turned[:, t, :], slots[:, t:N:PACK], identity[:])
+            nc.scalar.activation(
+                group.rearrange("p (e t) -> p e t", t=PACK), turned[:].rearrange("p t e -> p e t"), COPY
             )
-            v_codes[e, b] = codes
-            v_scales[e, b] = scales
 
-        sums = {}
+        v0_slots = keep.tile([P, B * N], F32, name="v0_slots")
+        v0_group = keep.tile([P, B * N], BF16, name="v0_group", align_bytes=64)
+        v1_groups = {}
+        v1_slots = {}
 
-        def finish(e, b):
-            if b not in sums:
-                total = out_pool.tile([P, DV], F32, name="total")
-                sums[b] = total
-            cols = slice(e * P, (e + 1) * P)
-            nc.tensor.matmul_mx(
-                out=sums[b][:, cols],
-                lhsT=w_codes[b][:].bitcast(FP8X4),
-                lhsT_scale=w_scales[b][:],
-                rhs=v_codes[e, b][:].bitcast(FP8X4),
-                rhs_scale=v_scales[e, b][:],
-                start=True,
-                stop=True,
-            )
-            result = keep.tile([P, P], F32, name=f"result_{e}_{b}")
-            nc.scalar.activation(result[:], sums[b][:, cols], COPY, scale=1.0 / 16.0)
-            nc.sync.dma_start(out[b, :, cols], result[:])
+        def gather_last_values(b):
+            slots = keep.tile([P, N], F32, name=f"v1_slots_{b}")
+            nc.vector.tensor_copy(slots[:], v_raw[1][:].indirect(offsets(b)))
+            v1_slots[b] = slots
 
-        gather_values(0, 0)
-        turn_values(0, 0)
-        gather_values(0, 1)
-        turn_values(0, 1)
+        def turn_last_values(b):
+            group = keep.tile([P, N], BF16, name=f"v1_group_{b}", align_bytes=64)
+            turn_values(v1_slots[b][:], group[:])
+            v1_groups[b] = group
+
+        def quantise_last_values(b):
+            mx["v1", b] = quantise(f"v1_{b}", v1_groups[b][:], P)
+
+        totals = {}
+
+        def first_products(b):
+            total = out_pool.tile([P, DV], F32, name="total")
+            totals[b] = total
+            multiply(total[:, block(0)], mx["w", b], block(0), mx["v0"], block(b))
+
+        def finish(b):
+            multiply(totals[b][:, block(1)], mx["w", b], block(0), mx["v1", b], block(0))
+            result = keep.tile([P, DV], F32, name=f"result_{b}")
+            if b == 0:
+                nc.vector.tensor_scalar(result[:], totals[b][:], 1.0 / 16.0, None, MULT)
+            else:
+                nc.scalar.activation(result[:], totals[b][:], COPY, scale=1.0 / 16.0)
+            nc.sync.dma_start(out[b], result[:])
+
+        round_queries()
         token_scales()
-        quantise_values(0, 0)
-        quantise_values(0, 1)
-        cast_keys(0)
-        queries()
-        gather_keys(0, 0)
-        gather_keys(0, 1)
-        cast_keys(1)
+        cast_keys(0, 0)
+        cast_keys(0, 1)
+        cast_keys(0, 2)
+        nc.vector.tensor_copy(k_words[:, 0], k_pairs[0][:].bitcast(U32).indirect(lists[:]))
+        quantise_queries()
+        cast_keys(1, 0)
+        cast_keys(1, 1)
+        cast_keys(1, 2)
         gather_keys(1, 0)
+        gather_keys(1, 1)
+        interleave_keys(0)
+        interleave_keys(1)
+        nc.vector.tensor_copy(v0_slots[:], v_raw[0][:].indirect(lists[:]))
         quantise_keys(0)
         scores(0)
-        gather_keys(1, 1)
+        turn_values(v0_slots[:, :N], v0_group[:, :N])
+        turn_values(v0_slots[:, N:], v0_group[:, N:])
+        gather_last_values(0)
         quantise_keys(1)
         scores(1)
+        gather_last_values(1)
+        turn_last_values(0)
+        turn_last_values(1)
         weigh(0)
+        mx["v0"] = quantise("v0", v0_group[:], B * P)
         quantise_weights(0)
-        finish(0, 0)
-        gather_values(1, 0)
-        turn_values(1, 0)
+        first_products(0)
         weigh(1)
+        quantise_last_values(0)
+        finish(0)
         quantise_weights(1)
-        finish(0, 1)
-        gather_values(1, 1)
-        turn_values(1, 1)
-        quantise_values(1, 0)
-        finish(1, 0)
-        quantise_values(1, 1)
-        finish(1, 1)
+        first_products(1)
+        quantise_last_values(1)
+        finish(1)

from contextlib import ExitStack

import concourse.mybir as mybir
from concourse.masks import make_identity

B, N, T, D, DV, NQ = 2, 512, 2048, 512, 256, 128
P = 128
PACK = 4
LIST_COLS = N // 16
FLOPS = 2 * B * NQ * N * (D + DV)

F32 = mybir.dt.float32
BF16 = mybir.dt.bfloat16
U32 = mybir.dt.uint32
U16 = mybir.dt.uint16
U8 = mybir.dt.uint8
FP8X4 = mybir.dt.float8_e4m3fn_x4
COPY = mybir.ActivationFunctionType.Copy
SILU = mybir.ActivationFunctionType.Silu
MULT = mybir.AluOpType.mult

K_SHARES = (((448, 64), (448, 64), (640, 384)), ((832, 192), (192, 320), (320, 192)))


def tile_attend_x_silu_kernel(tc, qT, kT, vT, vs, offs, out):
    nc = tc.nc
    with ExitStack() as ctx:
        keep = ctx.enter_context(tc.tile_pool(name="keep", bufs=1))
        scale_pool = ctx.enter_context(tc.psum_pool(name="scale", bufs=2))
        turn_pool = ctx.enter_context(tc.psum_pool(name="turn", bufs=2))
        score_pool = ctx.enter_context(tc.psum_pool(name="score", bufs=2))
        out_pool = ctx.enter_context(tc.psum_pool(name="outs", bufs=2))

        lists = keep.tile([P, B * LIST_COLS], U16, name="lists")
        nc.sync.dma_start(lists[:], offs)

        vs_row = keep.tile([P, T], F32, name="vs_row")
        nc.vector.memset(vs_row[:, : T // 2], 0.0)
        nc.gpsimd.memset(vs_row[:, T // 2 :], 0.0)
        identity = keep.tile([P, P], F32, name="identity")
        make_identity(nc, identity[:])
        warm = keep.tile([P, 1], F32, name="warm")
        nc.vector.memset(warm[:], 0.0)
        nc.scalar.activation(warm[:], warm[:], SILU)

        k_rows = kT.rearrange("(p j) w -> p j w", j=PACK)
        k_raw = {}

        def load_keys(u, c):
            start = sum(a + b for a, b in K_SHARES[u][:c])
            width = sum(K_SHARES[u][c])
            raw = keep.tile([P, 2, width], F32, name=f"k_raw_{u}_{c}")
            nc.sync.dma_start(raw[:], k_rows[:, 2 * u : 2 * u + 2, start : start + width])
            k_raw[u, c] = raw

        v_raw = {}

        def load_values(e):
            raw = keep.tile([P, T], F32, name=f"v_raw_{e}")
            nc.sync.dma_start(raw[:], vT[e * P : (e + 1) * P, :])
            v_raw[e] = raw

        q_raw = keep.tile([P, B, PACK, NQ], F32, name="q_raw")
        nc.sync.dma_start(q_raw[:], qT.rearrange("b (p j) q -> p b j q", j=PACK))
        load_keys(0, 0)
        nc.sync.dma_start(vs_row[0:1, :], vs[0:1, :])
        load_keys(0, 1)
        load_keys(0, 2)
        load_keys(1, 0)
        load_keys(1, 1)
        load_keys(1, 2)
        load_values(0)
        load_values(1)

        k_pairs = []
        for u in range(2):
            pair = keep.tile([P, T * 2], BF16, name=f"k_pair_{u}")
            k_pairs.append(pair)

        def cast_keys(u, c):
            start = sum(a + b for a, b in K_SHARES[u][:c])
            on_scalar, on_vector = K_SHARES[u][c]
            dst = k_pairs[u][:, 2 * start : 2 * (start + on_scalar + on_vector)].rearrange("p (w j) -> p w j", j=2)
            src = k_raw[u, c][:].rearrange("p j w -> p w j")
            if on_scalar:
                nc.scalar.activation(dst[:, :on_scalar], src[:, :on_scalar], COPY)
            if on_vector:
                nc.vector.tensor_copy(dst[:, on_scalar:], src[:, on_scalar:])

        def offsets(b):
            return lists[:, b * LIST_COLS : (b + 1) * LIST_COLS]

        k_slots = keep.tile([P, 2 * B * N], U32, name="k_slots")
        k_words = k_slots[:].rearrange("p (u b t s) -> p u b s t", u=2, b=B, t=PACK)
        k_groups = []
        for b in range(B):
            group = keep.tile([P, N * PACK], BF16, name=f"k_group_{b}", align_bytes=64)
            k_groups.append(group)

        def interleave_keys(b):
            nc.scalar.copy(
                k_groups[b][:].rearrange("p (n u j) -> p n u j", u=2, j=2),
                k_slots[:].bitcast(BF16).rearrange("p (u b n j) -> p b n u j", u=2, b=B, j=2)[:, b],
            )

        def quantise(name, values, columns):
            codes = keep.tile([P, columns], U32, name=f"{name}_codes", align_bytes=64)
            scales = keep.tile([P, columns], U8, name=f"{name}_scales", align_bytes=64)
            nc.vector.quantize_mx(out=codes[:].bitcast(FP8X4), scales=scales[:], in_=values)
            return codes, scales

        mx = {}
        probs = {}
        w_groups = {}
        vs_turned = {}

        def token_scales():
            vs_slots = keep.tile([P, B * N], F32, name="vs_slots")
            nc.vector.tensor_copy(vs_slots[:], vs_row[:].indirect(lists[:]))
            for b in range(B):
                turned = scale_pool.tile([P, PACK, P], F32, name="scale_turned")
                for t in range(PACK):
                    nc.tensor.transpose(turned[:, t, :], vs_slots[:, b * N + t : (b + 1) * N : PACK], identity[:])
                vs_turned[b] = turned

        q_group = keep.tile([P, B * NQ * PACK], BF16, name="q_group", align_bytes=64)

        def round_queries():
            nc.gpsimd.tensor_scalar(
                q_group[:].rearrange("p (b q j) -> p b q j", b=B, j=PACK),
                q_raw[:].rearrange("p b j q -> p b q j"),
                1.0,
                0.0,
                MULT,
                mybir.AluOpType.add,
            )

        def quantise_queries():
            mx["q"] = quantise("q", q_group[:], B * NQ)

        def gather_keys(u, b):
            nc.vector.tensor_copy(k_words[:, u, b], k_pairs[u][:].bitcast(U32).indirect(offsets(b)))

        def quantise_keys(b):
            mx["k", b] = quantise(f"k_{b}", k_groups[b][:], N)

        def multiply(out_cols, left, left_cols, right, right_cols):
            nc.tensor.matmul_mx(
                out=out_cols,
                lhsT=left[0][:, left_cols].bitcast(FP8X4),
                lhsT_scale=left[1][:, left_cols],
                rhs=right[0][:, right_cols].bitcast(FP8X4),
                rhs_scale=right[1][:, right_cols],
                start=True,
                stop=True,
            )

        def block(i):
            return slice(i * P, (i + 1) * P)

        def scores(b):
            acc = score_pool.tile([P, PACK, NQ], F32, name="acc")
            for t in range(PACK):
                multiply(acc[:, t, :], mx["k", b], block(t), mx["q"], block(b))
            prob = keep.tile([P, PACK, NQ], F32, name=f"prob_{b}")
            nc.scalar.activation(prob[:], acc[:], SILU)
            probs[b] = prob

        def weigh(b):
            group = keep.tile([P, NQ, PACK], BF16, name=f"w_group_{b}", align_bytes=64)
            nc.vector.tensor_tensor(
                group[:],
                probs[b][:].rearrange("p t q -> p q t"),
                vs_turned[b][:, :, 0].unsqueeze(1).to_broadcast([P, NQ, PACK]),
                MULT,
            )
            w_groups[b] = group

        def quantise_weights(b):
            mx["w", b] = quantise(f"w_{b}", w_groups[b][:].rearrange("p q t -> p (q t)"), NQ)

        def turn_values(slots, group):
            turned = turn_pool.tile([P, PACK, P], F32, name="turned")
            for t in range(PACK):
                nc.tensor.transpose(turned[:, t, :], slots[:, t:N:PACK], identity[:])
            nc.scalar.activation(
                group.rearrange("p (e t) -> p e t", t=PACK), turned[:].rearrange("p t e -> p e t"), COPY
            )

        v0_slots = keep.tile([P, B * N], F32, name="v0_slots")
        v0_group = keep.tile([P, B * N], BF16, name="v0_group", align_bytes=64)
        v1_groups = {}
        v1_slots = {}

        def gather_last_values(b):
            slots = keep.tile([P, N], F32, name=f"v1_slots_{b}")
            nc.vector.tensor_copy(slots[:], v_raw[1][:].indirect(offsets(b)))
            v1_slots[b] = slots

        def turn_last_values(b):
            group = keep.tile([P, N], BF16, name=f"v1_group_{b}", align_bytes=64)
            turn_values(v1_slots[b][:], group[:])
            v1_groups[b] = group

        def quantise_last_values(b):
            mx["v1", b] = quantise(f"v1_{b}", v1_groups[b][:], P)

        totals = {}

        def first_products(b):
            total = out_pool.tile([P, DV], F32, name="total")
            totals[b] = total
            multiply(total[:, block(0)], mx["w", b], block(0), mx["v0"], block(b))

        def finish(b):
            multiply(totals[b][:, block(1)], mx["w", b], block(0), mx["v1", b], block(0))
            result = keep.tile([P, DV], F32, name=f"result_{b}")
            if b == 0:
                nc.vector.tensor_scalar(result[:], totals[b][:], 1.0 / 16.0, None, MULT)
            else:
                nc.scalar.activation(result[:], totals[b][:], COPY, scale=1.0 / 16.0)
            nc.sync.dma_start(out[b], result[:])

        round_queries()
        token_scales()
        cast_keys(0, 0)
        cast_keys(0, 1)
        cast_keys(0, 2)
        nc.vector.tensor_copy(k_words[:, 0], k_pairs[0][:].bitcast(U32).indirect(lists[:]))
        quantise_queries()
        cast_keys(1, 0)
        cast_keys(1, 1)
        cast_keys(1, 2)
        gather_keys(1, 0)
        gather_keys(1, 1)
        interleave_keys(0)
        interleave_keys(1)
        nc.vector.tensor_copy(v0_slots[:], v_raw[0][:].indirect(lists[:]))
        quantise_keys(0)
        scores(0)
        turn_values(v0_slots[:, :N], v0_group[:, :N])
        turn_values(v0_slots[:, N:], v0_group[:, N:])
        gather_last_values(0)
        quantise_keys(1)
        scores(1)
        gather_last_values(1)
        turn_last_values(0)
        turn_last_values(1)
        weigh(0)
        mx["v0"] = quantise("v0", v0_group[:], B * P)
        quantise_weights(0)
        first_products(0)
        weigh(1)
        quantise_last_values(0)
        finish(0)
        quantise_weights(1)
        first_products(1)
        quantise_last_values(1)
        finish(1)
